import numpy as np
import ml_dtypes


def mxq(x, axis, fmt="e4m3"):
    dtype, down = {"e4m3": (ml_dtypes.float8_e4m3fn, 7), "e5m2": (ml_dtypes.float8_e5m2, 14)}[fmt]
    v = np.moveaxis(np.asarray(x, np.float32).astype(ml_dtypes.bfloat16).astype(np.float64), axis, -1)
    blocks = v.reshape(v.shape[:-1] + (-1, 32))
    amax = np.abs(blocks).max(-1, keepdims=True)
    byte = np.maximum(np.where(amax > 0, np.frexp(amax)[1] - 1 + 127, 0) - down, 1)
    scale = np.exp2(byte - 127.0)
    codes = (blocks / scale).astype(np.float32).astype(dtype).astype(np.float64)
    return np.moveaxis((codes * scale).reshape(v.shape), -1, axis)


WIDE = False


def mx_kscale(k):
    if not WIDE:
        return np.ones(k)
    levels = np.array([10, -10, 5, -5, 0])
    if k % 512:
        return np.exp2(np.random.permutation(np.resize(levels, k // 32))).repeat(32)
    a = np.empty((k // 512, 16))
    for p in range(k // 512):
        a[p, :8] = np.random.permutation(np.resize(levels, 8))
        for g in range(8):
            far = levels[np.abs(levels - a[p, g]) >= 10]
            a[p, g + 8] = far[np.random.randint(len(far))]
    return np.exp2(a.ravel()).repeat(32)


def f64(x):
    return np.asarray(x).astype(np.float64)


def striped8(idx):
    return np.asarray(idx).reshape(8, -1, 16).transpose(0, 2, 1).reshape(128, -1).astype(np.uint16)


def unstriped8(offs):
    return offs.reshape(8, 16, -1).transpose(0, 2, 1).reshape(8, -1).astype(np.int64)


def pick8(x, idx, run):
    r = np.arange(len(x))
    return x[r[:, None], idx[r % (8 * run) // run]]


E2M1 = np.array([0.0, 0.5, 1.0, 1.5, 2.0, 3.0, 4.0, 6.0, -0.0, -0.5, -1.0, -1.5, -2.0, -3.0, -4.0, -6.0])


def pack_weight(w, fmt):
    k, n = w.shape
    w = f64(np.asarray(w, np.float32).astype(ml_dtypes.bfloat16)).reshape(k // 32, 32, n)
    amax = np.abs(w).max(1)
    if fmt == "e4m3":
        byte = np.frexp(amax)[1] - 1 + 127 - 7
    else:
        mant, ex = np.frexp(amax / 6.0)
        byte = np.where(mant > 0.5, ex, ex - 1) + 127
    byte = np.clip(np.where(amax > 0, byte, 1), 1, 254)
    scaled = (w * np.exp2(127.0 - byte)[:, None, :]).reshape(k, n).astype(np.float32)
    by_word = np.ascontiguousarray(scaled.reshape(k // 512, 128, 4, n).transpose(0, 1, 3, 2))
    if fmt == "e4m3":
        words = by_word.astype(ml_dtypes.float8_e4m3fn).view(np.uint8)
    else:
        c = by_word.astype(ml_dtypes.float4_e2m1fn).view(np.uint8) & 0xF
        words = (c[..., 0::2] | (c[..., 1::2] << 4)).reshape(k // 512, 128, 2 * n)
    return np.ascontiguousarray(words), np.ascontiguousarray(byte.astype(np.uint8).reshape(k // 512, 16, n))


def unpack_weight(words, scales, fmt):
    g, _, n = scales.shape
    words = np.ascontiguousarray(words).reshape(g, 128, n, -1)
    if fmt == "e4m3":
        vals = words.view(ml_dtypes.float8_e4m3fn).astype(np.float64)
    else:
        nib = np.empty((g, 128, n, 4), np.uint8)
        nib[..., 0::2] = words & 0xF
        nib[..., 1::2] = words >> 4
        vals = E2M1[nib]
    vals = vals * np.repeat(np.exp2(scales.astype(np.float64) - 127.0), 8, axis=1)[..., None]
    return vals.transpose(0, 1, 3, 2).reshape(g * 512, n)


D, T, U, I, Q = 512, 1024, 1024, 512, 128


def setup_inputs():
    n = np.random.standard_normal
    idx = np.stack([np.random.permutation(T)[:I] for _ in range(8)])
    idx2 = np.stack([np.random.permutation(U)[:I] for _ in range(8)])
    idx3 = np.stack([np.random.permutation(T)[:I] for _ in range(8)])
    idx4 = np.stack([np.random.permutation(T)[:I] for _ in range(8)])
    idx5 = np.stack([np.random.permutation(U)[:I] for _ in range(8)])
    fd = mx_kscale(D)
    keysp = pack_weight(n((D, T)) / fd[:, None], "e4m3")
    notesp = pack_weight(n((D, U)) / fd[:, None], "e2m1")
    return {
        "query": (n((D, Q)) * 1.0 / np.sqrt(D) * fd[:, None]).astype(np.float32),
        "keys_words": keysp[0],
        "keys_scales": keysp[1],
        "notes_words": notesp[0],
        "notes_scales": notesp[1],
        "offs": striped8(idx),
        "offs2": striped8(idx2),
        "offs3": striped8(idx3),
        "offs4": striped8(idx4),
        "offs5": striped8(idx5),
    }


def reference(query, keys_words, keys_scales, notes_words, notes_scales, offs, offs2, offs3, offs4, offs5):
    idx = unstriped8(offs)
    idx2 = unstriped8(offs2)
    idx3 = unstriped8(offs3)
    idx4 = unstriped8(offs4)
    idx5 = unstriped8(offs5)
    keysu = unpack_weight(keys_words, keys_scales, "e4m3")
    notesu = unpack_weight(notes_words, notes_scales, "e2m1")
    queryq = mxq(f64(query), 0, "e4m3")
    a = queryq.T @ keysu
    b = queryq.T @ notesu
    r = pick8(a, idx, 16) - pick8(b, idx2, 16)
    f1 = np.zeros((Q, T))
    f1[np.arange(Q)[:, None], idx3[np.arange(Q) % 128 // 16]] = r
    c1 = a + f1
    w = np.maximum(pick8(c1, idx4, 16), pick8(b, idx5, 16))
    y = w - r
    return y

@@ -1,0 +1,113 @@
+from contextlib import ExitStack
+
+import concourse.mybir as mybir
+
+D, T, U, I, Q = 512, 1024, 1024, 512, 128
+FLOPS = 2 * D * Q * (T + U)
+
+F32 = mybir.dt.float32
+BF16 = mybir.dt.bfloat16
+I32 = mybir.dt.int32
+U32 = mybir.dt.uint32
+U16 = mybir.dt.uint16
+U8 = mybir.dt.uint8
+FP8X4 = mybir.dt.float8_e4m3fn_x4
+FP4X4 = mybir.dt.float4_e2m1fn_x4
+ALU = mybir.AluOpType
+COPY = mybir.ActivationFunctionType.Copy
+
+P = 128
+PACK = 4
+PIECE = 256
+HALF = I // 2
+KEY_ROW = 4
+
+
+def tile_attend_sidelooks_two_kernel(tc, query, keys_words, keys_scales, notes_words, notes_scales,
+                                      offs, offs2, offs3, offs4, offs5, out):
+    nc = tc.nc
+    with ExitStack() as ctx:
+        lists = ctx.enter_context(tc.tile_pool(name="lists", bufs=1))
+        sb = ctx.enter_context(tc.tile_pool(name="sb", bufs=1))
+        psum = ctx.enter_context(tc.psum_pool(name="psum", bufs=1))
+
+        note_plane = sb.tile([P, U], U8, align_bytes=64)
+        key_plane = sb.tile([P, T], U8, align_bytes=64)
+        f1 = sb.tile([P, T], F32, align_bytes=64)
+        nc.vector.memset(note_plane[:].bitcast(I32), 0)
+        nc.vector.memset(key_plane[:].bitcast(I32), 0)
+        nc.vector.memset(f1[:], 0.0)
+
+        q_raw = sb.tile([P, PACK, Q], F32, align_bytes=64)
+        nc.sync.dma_start(out=q_raw[:], in_=query.rearrange("(p j) q -> p j q", j=PACK))
+        note_rows = notes_scales[0].bitcast(I32).rearrange("(g r) c -> r g c", r=4)
+        key_rows = keys_scales[0].bitcast(I32).rearrange("(g r) c -> r g c", r=4)
+        for r in range(4):
+            nc.scalar.dma_start(out=note_plane[r:P:32, :].bitcast(I32), in_=note_rows[r])
+        note_words = sb.tile([P, 2 * U], U8, align_bytes=64)
+        nc.sync.dma_start(out=note_words[:].bitcast(I32), in_=notes_words[0].bitcast(I32))
+        key_words = sb.tile([P, T], U32, align_bytes=64)
+        nc.sync.dma_start(out=key_words[:].bitcast(I32),
+                          in_=keys_words[0].rearrange("p n t -> p (n t)").bitcast(I32))
+        for r in range(4):
+            nc.sync.dma_start(out=key_plane[KEY_ROW + r:P:32, :].bitcast(I32), in_=key_rows[r])
+        held = {}
+        for name, src in (("offs2", offs2), ("offs", offs), ("offs3", offs3), ("offs5", offs5), ("offs4", offs4)):
+            held[name] = lists.tile([P, I // 16], U16, name=name)
+            nc.sync.dma_start(held[name][:], src)
+
+        def half(name, h):
+            return held[name][:, h * HALF // 16:(h + 1) * HALF // 16]
+
+        q_bf = sb.tile([P, Q, PACK], BF16, align_bytes=64)
+        nc.vector.tensor_copy(out=q_bf[:].rearrange("p (c i) t -> p c t i", i=4),
+                              in_=q_raw[:].rearrange("p t (c i) -> p c t i", i=4))
+        q_codes = sb.tile([P, Q], U32, align_bytes=64)
+        q_plane = sb.tile([P, Q], U8, align_bytes=64)
+        nc.vector.quantize_mx(out=q_codes[:].bitcast(FP8X4), scales=q_plane[:],
+                              in_=q_bf[:].rearrange("p q t -> p (q t)"))
+
+        b = sb.tile([P, U], F32, align_bytes=64)
+        for c0 in range(0, U, PIECE):
+            bank = psum.tile([P, PIECE], F32, name="b%d" % c0)
+            nc.tensor.matmul_mx(out=bank[:], lhsT=q_codes[:].bitcast(FP8X4), lhsT_scale=q_plane[:],
+                                rhs=note_words[:, 2 * c0:2 * (c0 + PIECE)].bitcast(FP4X4),
+                                rhs_scale=note_plane[:, c0:c0 + PIECE], start=True, stop=True)
+            nc.scalar.activation(b[:, c0:c0 + PIECE], bank[:], COPY)
+        a = sb.tile([P, T], F32, align_bytes=64)
+        for c0 in range(0, T, PIECE):
+            bank = psum.tile([P, PIECE], F32, name="a%d" % c0)
+            nc.tensor.matmul_mx(out=bank[:], lhsT=q_codes[:].bitcast(FP8X4), lhsT_scale=q_plane[:],
+                                rhs=key_words[:, c0:c0 + PIECE].bitcast(FP8X4),
+                                rhs_scale=key_plane[KEY_ROW:P, c0:c0 + PIECE], start=True, stop=True)
+            nc.vector.tensor_copy(a[:, c0:c0 + PIECE], bank[:])
+
+        def halves(name):
+            return [sb.tile([P, HALF], F32, name="%s%d" % (name, h), align_bytes=64) for h in range(2)]
+
+        b2 = halves("b2")
+        r = halves("r")
+        for h in range(2):
+            nc.scalar.activation(b2[h][:], b[:].indirect(half("offs2", h)), COPY)
+        a1 = sb.tile([P, HALF], F32, align_bytes=64)
+        nc.scalar.activation(a1[:], a[:].indirect(half("offs", 1)), COPY)
+        nc.vector.tensor_tensor(r[0][:], a[:].indirect(half("offs", 0)), b2[0][:], ALU.subtract)
+        nc.vector.tensor_tensor(r[1][:], a1[:], b2[1][:], ALU.subtract)
+        for h in range(2):
+            nc.vector.tensor_copy(f1[:].indirect(half("offs3", h)), r[h][:])
+        b5 = halves("b2")
+        for h in range(2):
+            nc.scalar.activation(b5[h][:], b[:].indirect(half("offs5", h)), COPY)
+
+        c1 = sb.tile([P, T], F32, align_bytes=64)
+        nc.vector.tensor_tensor(c1[:], a[:], f1[:], ALU.add)
+        c4 = halves("c4")
+        nc.vector.tensor_copy(c4[0][:], c1[:].indirect(half("offs4", 0)))
+        nc.scalar.activation(c4[1][:], c1[:].indirect(half("offs4", 1)), COPY)
+        w = halves("w")
+        y = halves("y")
+        for h in (1, 0):
+            nc.vector.tensor_tensor(w[h][:], c4[h][:], b5[h][:], ALU.max)
+        for h in (1, 0):
+            nc.vector.tensor_tensor(y[h][:], w[h][:], r[h][:], ALU.subtract)
+            nc.sync.dma_start(out=out[:, h * HALF:(h + 1) * HALF], in_=y[h][:])

@@ -42,10 +42,11 @@ def tile_attend_sidelooks_two_kernel(tc, query, keys_words, keys_scales, notes_w
         nc.sync.dma_start(out=q_raw[:], in_=query.rearrange("(p j) q -> p j q", j=PACK))
         note_rows = notes_scales[0].bitcast(I32).rearrange("(g r) c -> r g c", r=4)
         key_rows = keys_scales[0].bitcast(I32).rearrange("(g r) c -> r g c", r=4)
-        for r in range(4):
-            nc.scalar.dma_start(out=note_plane[r:P:32, :].bitcast(I32), in_=note_rows[r])
         note_words = sb.tile([P, 2 * U], U8, align_bytes=64)
-        nc.sync.dma_start(out=note_words[:].bitcast(I32), in_=notes_words[0].bitcast(I32))
+        for r in range(4):
+            if r == 2:
+                nc.sync.dma_start(out=note_words[:].bitcast(I32), in_=notes_words[0].bitcast(I32))
+            nc.sync.dma_start(out=note_plane[r:P:32, :].bitcast(I32), in_=note_rows[r])
         key_words = sb.tile([P, T], U32, align_bytes=64)
         nc.sync.dma_start(out=key_words[:].bitcast(I32),
                           in_=keys_words[0].rearrange("p n t -> p (n t)").bitcast(I32))
@@ -74,40 +75,39 @@ def tile_attend_sidelooks_two_kernel(tc, query, keys_words, keys_scales, notes_w
                                 rhs=note_words[:, 2 * c0:2 * (c0 + PIECE)].bitcast(FP4X4),
                                 rhs_scale=note_plane[:, c0:c0 + PIECE], start=True, stop=True)
             nc.scalar.activation(b[:, c0:c0 + PIECE], bank[:], COPY)
-        a = sb.tile([P, T], F32, align_bytes=64)
+        a = sb.tile([P, T], F32, name="a", align_bytes=64)
+        a_banks = []
         for c0 in range(0, T, PIECE):
             bank = psum.tile([P, PIECE], F32, name="a%d" % c0)
             nc.tensor.matmul_mx(out=bank[:], lhsT=q_codes[:].bitcast(FP8X4), lhsT_scale=q_plane[:],
                                 rhs=key_words[:, c0:c0 + PIECE].bitcast(FP8X4),
                                 rhs_scale=key_plane[KEY_ROW:P, c0:c0 + PIECE], start=True, stop=True)
-            nc.vector.tensor_copy(a[:, c0:c0 + PIECE], bank[:])
+            nc.scalar.activation(a[:, c0:c0 + PIECE], bank[:], COPY)
+            a_banks.append(bank)
 
         def halves(name):
             return [sb.tile([P, HALF], F32, name="%s%d" % (name, h), align_bytes=64) for h in range(2)]
 
-        b2 = halves("b2")
-        r = halves("r")
-        for h in range(2):
-            nc.scalar.activation(b2[h][:], b[:].indirect(half("offs2", h)), COPY)
-        a1 = sb.tile([P, HALF], F32, align_bytes=64)
-        nc.scalar.activation(a1[:], a[:].indirect(half("offs", 1)), COPY)
-        nc.vector.tensor_tensor(r[0][:], a[:].indirect(half("offs", 0)), b2[0][:], ALU.subtract)
-        nc.vector.tensor_tensor(r[1][:], a1[:], b2[1][:], ALU.subtract)
-        for h in range(2):
-            nc.vector.tensor_copy(f1[:].indirect(half("offs3", h)), r[h][:])
-        b5 = halves("b2")
-        for h in range(2):
-            nc.scalar.activation(b5[h][:], b[:].indirect(half("offs5", h)), COPY)
+        minus_b2 = sb.tile([P, I], F32, align_bytes=64)
+        nc.vector.tensor_scalar(minus_b2[:], b[:].indirect(held["offs2"][:]), -1.0, 0.0, ALU.mult, ALU.add)
+        r = sb.tile([P, I], F32, align_bytes=64)
+        nc.vector.tensor_copy(r[:, :HALF], a[:].indirect(half("offs", 0)))
+        nc.scalar.activation(r[:, HALF:], a[:].indirect(half("offs", 1)), COPY)
+        nc.vector.tensor_tensor(f1[:].indirect(held["offs3"][:]), r[:], minus_b2[:], ALU.add)
+        b5 = sb.tile([P, I], F32, name="a", align_bytes=64)
+        nc.scalar.activation(b5[:], b[:].indirect(held["offs5"][:]), COPY)
+        nc.gpsimd.tensor_tensor(r[:], r[:], minus_b2[:], ALU.add)
 
         c1 = sb.tile([P, T], F32, align_bytes=64)
-        nc.vector.tensor_tensor(c1[:], a[:], f1[:], ALU.add)
+        for k, c0 in enumerate(range(0, T, PIECE)):
+            nc.vector.tensor_tensor(c1[:, c0:c0 + PIECE], a_banks[k][:], f1[:, c0:c0 + PIECE], ALU.add)
         c4 = halves("c4")
         nc.vector.tensor_copy(c4[0][:], c1[:].indirect(half("offs4", 0)))
         nc.scalar.activation(c4[1][:], c1[:].indirect(half("offs4", 1)), COPY)
         w = halves("w")
         y = halves("y")
-        for h in (1, 0):
-            nc.vector.tensor_tensor(w[h][:], c4[h][:], b5[h][:], ALU.max)
-        for h in (1, 0):
-            nc.vector.tensor_tensor(y[h][:], w[h][:], r[h][:], ALU.subtract)
+        for h in range(2):
+            nc.vector.tensor_tensor(w[h][:], c4[h][:], b5[:, h * HALF:(h + 1) * HALF], ALU.max)
+        for h in range(2):
+            nc.vector.tensor_tensor(y[h][:], w[h][:], r[:, h * HALF:(h + 1) * HALF], ALU.subtract)
             nc.sync.dma_start(out=out[:, h * HALF:(h + 1) * HALF], in_=y[h][:])

@@ -1,6 +1,7 @@
 from contextlib import ExitStack
 
 import concourse.mybir as mybir
+from concourse.masks import make_identity
 
 D, T, U, I, Q = 512, 1024, 1024, 512, 128
 FLOPS = 2 * D * Q * (T + U)
@@ -60,21 +61,31 @@ def tile_attend_sidelooks_two_kernel(tc, query, keys_words, keys_scales, notes_w
         def half(name, h):
             return held[name][:, h * HALF // 16:(h + 1) * HALF // 16]
 
-        q_bf = sb.tile([P, Q, PACK], BF16, align_bytes=64)
-        nc.vector.tensor_copy(out=q_bf[:].rearrange("p (c i) t -> p c t i", i=4),
-                              in_=q_raw[:].rearrange("p t (c i) -> p c t i", i=4))
+        q_bf = sb.tile([P, Q, PACK], BF16, name="q_bf", align_bytes=64)
+        q_halves = [slice(0, Q // 2), slice(Q // 2, Q)]
+        for cols in q_halves:
+            nc.vector.tensor_copy(out=q_bf[:, cols, :].rearrange("p (c i) t -> p c t i", i=4),
+                                  in_=q_raw[:, :, cols].rearrange("p t (c i) -> p c t i", i=4))
         q_codes = sb.tile([P, Q], U32, align_bytes=64)
         q_plane = sb.tile([P, Q], U8, align_bytes=64)
-        nc.vector.quantize_mx(out=q_codes[:].bitcast(FP8X4), scales=q_plane[:],
-                              in_=q_bf[:].rearrange("p q t -> p (q t)"))
+        for cols in q_halves:
+            nc.vector.quantize_mx(out=q_codes[:, cols].bitcast(FP8X4), scales=q_plane[:, cols],
+                                  in_=q_bf[:, cols, :].rearrange("p q t -> p (q t)"))
 
+        identity = sb.tile([P, P], F32, name="q_bf", align_bytes=64)
+        make_identity(nc, identity[:])
         b = sb.tile([P, U], F32, align_bytes=64)
         for c0 in range(0, U, PIECE):
             bank = psum.tile([P, PIECE], F32, name="b%d" % c0)
             nc.tensor.matmul_mx(out=bank[:], lhsT=q_codes[:].bitcast(FP8X4), lhsT_scale=q_plane[:],
                                 rhs=note_words[:, 2 * c0:2 * (c0 + PIECE)].bitcast(FP4X4),
                                 rhs_scale=note_plane[:, c0:c0 + PIECE], start=True, stop=True)
-            nc.scalar.activation(b[:, c0:c0 + PIECE], bank[:], COPY)
+            if c0 // PIECE % 2 == 0:
+                nc.scalar.activation(b[:, c0:c0 + PIECE], bank[:], COPY)
+            else:
+                nc.vector.tensor_copy(b[:, c0:c0 + PIECE], bank[:])
+        minus_b2 = sb.tile([P, I], F32, align_bytes=64)
+        nc.vector.tensor_scalar(minus_b2[:], b[:].indirect(held["offs2"][:]), -1.0, 0.0, ALU.mult, ALU.add)
         a = sb.tile([P, T], F32, name="a", align_bytes=64)
         a_banks = []
         for c0 in range(0, T, PIECE):
@@ -88,26 +99,36 @@ def tile_attend_sidelooks_two_kernel(tc, query, keys_words, keys_scales, notes_w
         def halves(name):
             return [sb.tile([P, HALF], F32, name="%s%d" % (name, h), align_bytes=64) for h in range(2)]
 
-        minus_b2 = sb.tile([P, I], F32, align_bytes=64)
-        nc.vector.tensor_scalar(minus_b2[:], b[:].indirect(held["offs2"][:]), -1.0, 0.0, ALU.mult, ALU.add)
-        r = sb.tile([P, I], F32, align_bytes=64)
-        nc.vector.tensor_copy(r[:, :HALF], a[:].indirect(half("offs", 0)))
-        nc.scalar.activation(r[:, HALF:], a[:].indirect(half("offs", 1)), COPY)
-        nc.vector.tensor_tensor(f1[:].indirect(held["offs3"][:]), r[:], minus_b2[:], ALU.add)
-        b5 = sb.tile([P, I], F32, name="a", align_bytes=64)
-        nc.scalar.activation(b5[:], b[:].indirect(held["offs5"][:]), COPY)
-        nc.gpsimd.tensor_tensor(r[:], r[:], minus_b2[:], ALU.add)
+        a1 = sb.tile([P, I], F32, align_bytes=64)
+        nc.vector.tensor_copy(a1[:, :HALF], a[:].indirect(half("offs", 0)))
+        nc.scalar.activation(a1[:, HALF:], a[:].indirect(half("offs", 1)), COPY)
+        nc.vector.tensor_tensor(f1[:].indirect(held["offs3"][:]), a1[:], minus_b2[:], ALU.add)
+        late = sb.tile([P, I + PIECE], F32, name="a", align_bytes=64)
+        b5 = late[:, :I]
+        a_last = late[:, I:]
+        nc.scalar.activation(a_last, a_banks[-1][:], COPY)
+        nc.scalar.activation(b5, b[:].indirect(held["offs5"][:]), COPY)
+        turned = psum.tile([P, I], F32, name="b0")
+        for s0 in range(0, I, P):
+            for k, term in enumerate((minus_b2, a1)):
+                nc.tensor.matmul(turned[:, s0:s0 + P], term[:, s0:s0 + P], identity[:],
+                                 start=(k == 0), stop=(k == 1), is_transpose=True)
+        r_turned = sb.tile([P, I], F32, name="c4", align_bytes=64)
+        nc.scalar.activation(r_turned[:], turned[:], COPY)
+        r = psum.tile([P, I], F32, name="b256")
+        for s0 in range(0, I, P):
+            nc.tensor.transpose(r[:, s0:s0 + P], r_turned[:, s0:s0 + P], identity[:])
 
         c1 = sb.tile([P, T], F32, align_bytes=64)
-        for k, c0 in enumerate(range(0, T, PIECE)):
+        nc.gpsimd.tensor_tensor(c1[:, T - PIECE:], a_last, f1[:, T - PIECE:], ALU.add)
+        for k, c0 in enumerate(range(0, T - PIECE, PIECE)):
             nc.vector.tensor_tensor(c1[:, c0:c0 + PIECE], a_banks[k][:], f1[:, c0:c0 + PIECE], ALU.add)
-        c4 = halves("c4")
-        nc.vector.tensor_copy(c4[0][:], c1[:].indirect(half("offs4", 0)))
-        nc.scalar.activation(c4[1][:], c1[:].indirect(half("offs4", 1)), COPY)
-        w = halves("w")
+        c4 = sb.tile([P, I], F32, name="c4", align_bytes=64)
+        nc.vector.tensor_copy(c4[:, :HALF], c1[:].indirect(half("offs4", 0)))
+        nc.scalar.activation(c4[:, HALF:], c1[:].indirect(half("offs4", 1)), COPY)
+        w = sb.tile([P, I], F32, align_bytes=64)
         y = halves("y")
+        nc.vector.tensor_tensor(w[:], c4[:], b5, ALU.max)
         for h in range(2):
-            nc.vector.tensor_tensor(w[h][:], c4[h][:], b5[:, h * HALF:(h + 1) * HALF], ALU.max)
-        for h in range(2):
-            nc.vector.tensor_tensor(y[h][:], w[h][:], r[:, h * HALF:(h + 1) * HALF], ALU.subtract)
+            nc.vector.tensor_tensor(y[h][:], w[:, h * HALF:(h + 1) * HALF], r[:, h * HALF:(h + 1) * HALF], ALU.subtract)
             nc.sync.dma_start(out=out[:, h * HALF:(h + 1) * HALF], in_=y[h][:])

@@ -19,9 +19,13 @@ COPY = mybir.ActivationFunctionType.Copy
 
 P = 128
 PACK = 4
+QUADRANT = 32
+ROWS = 4
+GROUP = 16
 PIECE = 256
 HALF = I // 2
 KEY_ROW = 4
+NOTE_ROWS_FIRST = 2
 
 
 def tile_attend_sidelooks_two_kernel(tc, query, keys_words, keys_scales, notes_words, notes_scales,
@@ -40,26 +44,26 @@ def tile_attend_sidelooks_two_kernel(tc, query, keys_words, keys_scales, notes_w
         nc.vector.memset(f1[:], 0.0)
 
         q_raw = sb.tile([P, PACK, Q], F32, align_bytes=64)
-        nc.sync.dma_start(out=q_raw[:], in_=query.rearrange("(p j) q -> p j q", j=PACK))
-        note_rows = notes_scales[0].bitcast(I32).rearrange("(g r) c -> r g c", r=4)
-        key_rows = keys_scales[0].bitcast(I32).rearrange("(g r) c -> r g c", r=4)
+        nc.sync.dma_start(out=q_raw[:], in_=query.rearrange("(p t) q -> p t q", t=PACK))
+        note_rows = notes_scales[0].bitcast(I32).rearrange("(g row) c -> row g c", row=ROWS)
+        key_rows = keys_scales[0].bitcast(I32).rearrange("(g row) c -> row g c", row=ROWS)
         note_words = sb.tile([P, 2 * U], U8, align_bytes=64)
-        for r in range(4):
-            if r == 2:
+        for row in range(ROWS):
+            if row == NOTE_ROWS_FIRST:
                 nc.sync.dma_start(out=note_words[:].bitcast(I32), in_=notes_words[0].bitcast(I32))
-            nc.sync.dma_start(out=note_plane[r:P:32, :].bitcast(I32), in_=note_rows[r])
+            nc.sync.dma_start(out=note_plane[row:P:QUADRANT, :].bitcast(I32), in_=note_rows[row])
         key_words = sb.tile([P, T], U32, align_bytes=64)
         nc.sync.dma_start(out=key_words[:].bitcast(I32),
                           in_=keys_words[0].rearrange("p n t -> p (n t)").bitcast(I32))
-        for r in range(4):
-            nc.sync.dma_start(out=key_plane[KEY_ROW + r:P:32, :].bitcast(I32), in_=key_rows[r])
-        held = {}
+        for row in range(ROWS):
+            nc.sync.dma_start(out=key_plane[KEY_ROW + row:P:QUADRANT, :].bitcast(I32), in_=key_rows[row])
+        offsets = {}
         for name, src in (("offs2", offs2), ("offs", offs), ("offs3", offs3), ("offs5", offs5), ("offs4", offs4)):
-            held[name] = lists.tile([P, I // 16], U16, name=name)
-            nc.sync.dma_start(held[name][:], src)
+            offsets[name] = lists.tile([P, I // GROUP], U16, name=name)
+            nc.sync.dma_start(offsets[name][:], src)
 
-        def half(name, h):
-            return held[name][:, h * HALF // 16:(h + 1) * HALF // 16]
+        def half_list(name, h):
+            return offsets[name][:, h * HALF // GROUP:(h + 1) * HALF // GROUP]
 
         q_bf = sb.tile([P, Q, PACK], BF16, name="q_bf", align_bytes=64)
         q_halves = [slice(0, Q // 2), slice(Q // 2, Q)]
@@ -74,48 +78,49 @@ def tile_attend_sidelooks_two_kernel(tc, query, keys_words, keys_scales, notes_w
 
         identity = sb.tile([P, P], F32, name="q_bf", align_bytes=64)
         make_identity(nc, identity[:])
+
         b = sb.tile([P, U], F32, align_bytes=64)
-        for c0 in range(0, U, PIECE):
-            bank = psum.tile([P, PIECE], F32, name="b%d" % c0)
+        for k, c0 in enumerate(range(0, U, PIECE)):
+            bank = psum.tile([P, PIECE], F32, name="b_bank%d" % k)
             nc.tensor.matmul_mx(out=bank[:], lhsT=q_codes[:].bitcast(FP8X4), lhsT_scale=q_plane[:],
                                 rhs=note_words[:, 2 * c0:2 * (c0 + PIECE)].bitcast(FP4X4),
                                 rhs_scale=note_plane[:, c0:c0 + PIECE], start=True, stop=True)
-            if c0 // PIECE % 2 == 0:
+            if k % 2 == 0:
                 nc.scalar.activation(b[:, c0:c0 + PIECE], bank[:], COPY)
             else:
                 nc.vector.tensor_copy(b[:, c0:c0 + PIECE], bank[:])
+
         minus_b2 = sb.tile([P, I], F32, align_bytes=64)
-        nc.vector.tensor_scalar(minus_b2[:], b[:].indirect(held["offs2"][:]), -1.0, 0.0, ALU.mult, ALU.add)
+        nc.vector.tensor_scalar(minus_b2[:], b[:].indirect(offsets["offs2"][:]), -1.0, 0.0, ALU.mult, ALU.add)
         a = sb.tile([P, T], F32, name="a", align_bytes=64)
         a_banks = []
-        for c0 in range(0, T, PIECE):
-            bank = psum.tile([P, PIECE], F32, name="a%d" % c0)
+        for k, c0 in enumerate(range(0, T, PIECE)):
+            bank = psum.tile([P, PIECE], F32, name="a_bank%d" % k)
             nc.tensor.matmul_mx(out=bank[:], lhsT=q_codes[:].bitcast(FP8X4), lhsT_scale=q_plane[:],
                                 rhs=key_words[:, c0:c0 + PIECE].bitcast(FP8X4),
                                 rhs_scale=key_plane[KEY_ROW:P, c0:c0 + PIECE], start=True, stop=True)
             nc.scalar.activation(a[:, c0:c0 + PIECE], bank[:], COPY)
             a_banks.append(bank)
 
-        def halves(name):
-            return [sb.tile([P, HALF], F32, name="%s%d" % (name, h), align_bytes=64) for h in range(2)]
-
         a1 = sb.tile([P, I], F32, align_bytes=64)
-        nc.vector.tensor_copy(a1[:, :HALF], a[:].indirect(half("offs", 0)))
-        nc.scalar.activation(a1[:, HALF:], a[:].indirect(half("offs", 1)), COPY)
-        nc.vector.tensor_tensor(f1[:].indirect(held["offs3"][:]), a1[:], minus_b2[:], ALU.add)
-        late = sb.tile([P, I + PIECE], F32, name="a", align_bytes=64)
-        b5 = late[:, :I]
-        a_last = late[:, I:]
+        nc.vector.tensor_copy(a1[:, :HALF], a[:].indirect(half_list("offs", 0)))
+        nc.scalar.activation(a1[:, HALF:], a[:].indirect(half_list("offs", 1)), COPY)
+        nc.vector.tensor_tensor(f1[:].indirect(offsets["offs3"][:]), a1[:], minus_b2[:], ALU.add)
+
+        beside_scatter = sb.tile([P, I + PIECE], F32, name="a", align_bytes=64)
+        b5 = beside_scatter[:, :I]
+        a_last = beside_scatter[:, I:]
         nc.scalar.activation(a_last, a_banks[-1][:], COPY)
-        nc.scalar.activation(b5, b[:].indirect(held["offs5"][:]), COPY)
-        turned = psum.tile([P, I], F32, name="b0")
+        nc.scalar.activation(b5, b[:].indirect(offsets["offs5"][:]), COPY)
+
+        r_turned_bank = psum.tile([P, I], F32, name="b_bank0")
         for s0 in range(0, I, P):
             for k, term in enumerate((minus_b2, a1)):
-                nc.tensor.matmul(turned[:, s0:s0 + P], term[:, s0:s0 + P], identity[:],
+                nc.tensor.matmul(r_turned_bank[:, s0:s0 + P], term[:, s0:s0 + P], identity[:],
                                  start=(k == 0), stop=(k == 1), is_transpose=True)
-        r_turned = sb.tile([P, I], F32, name="c4", align_bytes=64)
-        nc.scalar.activation(r_turned[:], turned[:], COPY)
-        r = psum.tile([P, I], F32, name="b256")
+        r_turned = sb.tile([P, I], F32, name="r_turned", align_bytes=64)
+        nc.scalar.activation(r_turned[:], r_turned_bank[:], COPY)
+        r = psum.tile([P, I], F32, name="b_bank1")
         for s0 in range(0, I, P):
             nc.tensor.transpose(r[:, s0:s0 + P], r_turned[:, s0:s0 + P], identity[:])
 
@@ -123,12 +128,16 @@ def tile_attend_sidelooks_two_kernel(tc, query, keys_words, keys_scales, notes_w
         nc.gpsimd.tensor_tensor(c1[:, T - PIECE:], a_last, f1[:, T - PIECE:], ALU.add)
         for k, c0 in enumerate(range(0, T - PIECE, PIECE)):
             nc.vector.tensor_tensor(c1[:, c0:c0 + PIECE], a_banks[k][:], f1[:, c0:c0 + PIECE], ALU.add)
-        c4 = sb.tile([P, I], F32, name="c4", align_bytes=64)
-        nc.vector.tensor_copy(c4[:, :HALF], c1[:].indirect(half("offs4", 0)))
-        nc.scalar.activation(c4[:, HALF:], c1[:].indirect(half("offs4", 1)), COPY)
-        w = sb.tile([P, I], F32, align_bytes=64)
-        y = halves("y")
-        nc.vector.tensor_tensor(w[:], c4[:], b5, ALU.max)
-        for h in range(2):
-            nc.vector.tensor_tensor(y[h][:], w[:, h * HALF:(h + 1) * HALF], r[:, h * HALF:(h + 1) * HALF], ALU.subtract)
-            nc.sync.dma_start(out=out[:, h * HALF:(h + 1) * HALF], in_=y[h][:])
+
+        c4 = sb.tile([P, I], F32, name="r_turned", align_bytes=64)
+        nc.vector.tensor_copy(c4[:, :HALF], c1[:].indirect(half_list("offs4", 0)))
+        nc.scalar.activation(c4[:, HALF:], c1[:].indirect(half_list("offs4", 1)), COPY)
+
+        slot_halves = [slice(0, HALF), slice(HALF, I)]
+        w = [sb.tile([P, HALF], F32, name="w%d" % h, align_bytes=64) for h in range(2)]
+        y = [sb.tile([P, HALF], F32, name="y%d" % h, align_bytes=64) for h in range(2)]
+        for h, slots in enumerate(slot_halves):
+            nc.vector.tensor_tensor(w[h][:], c4[:, slots], b5[:, slots], ALU.max)
+        for h, slots in enumerate(slot_halves):
+            nc.vector.tensor_tensor(y[h][:], w[h][:], r[:, slots], ALU.subtract)
+            nc.sync.dma_start(out=out[:, slots], in_=y[h][:])

from contextlib import ExitStack

import concourse.mybir as mybir
from concourse.masks import make_identity

D, T, U, I, Q = 512, 1024, 1024, 512, 128
FLOPS = 2 * D * Q * (T + U)

F32 = mybir.dt.float32
BF16 = mybir.dt.bfloat16
I32 = mybir.dt.int32
U32 = mybir.dt.uint32
U16 = mybir.dt.uint16
U8 = mybir.dt.uint8
FP8X4 = mybir.dt.float8_e4m3fn_x4
FP4X4 = mybir.dt.float4_e2m1fn_x4
ALU = mybir.AluOpType
COPY = mybir.ActivationFunctionType.Copy

P = 128
PACK = 4
QUADRANT = 32
ROWS = 4
GROUP = 16
PIECE = 256
HALF = I // 2
KEY_ROW = 4
NOTE_ROWS_FIRST = 2


def tile_attend_sidelooks_two_kernel(tc, query, keys_words, keys_scales, notes_words, notes_scales,
                                      offs, offs2, offs3, offs4, offs5, out):
    nc = tc.nc
    with ExitStack() as ctx:
        lists = ctx.enter_context(tc.tile_pool(name="lists", bufs=1))
        sb = ctx.enter_context(tc.tile_pool(name="sb", bufs=1))
        psum = ctx.enter_context(tc.psum_pool(name="psum", bufs=1))

        note_plane = sb.tile([P, U], U8, align_bytes=64)
        key_plane = sb.tile([P, T], U8, align_bytes=64)
        f1 = sb.tile([P, T], F32, align_bytes=64)
        nc.vector.memset(note_plane[:].bitcast(I32), 0)
        nc.vector.memset(key_plane[:].bitcast(I32), 0)
        nc.vector.memset(f1[:], 0.0)

        q_raw = sb.tile([P, PACK, Q], F32, align_bytes=64)
        nc.sync.dma_start(out=q_raw[:], in_=query.rearrange("(p t) q -> p t q", t=PACK))
        note_rows = notes_scales[0].bitcast(I32).rearrange("(g row) c -> row g c", row=ROWS)
        key_rows = keys_scales[0].bitcast(I32).rearrange("(g row) c -> row g c", row=ROWS)
        note_words = sb.tile([P, 2 * U], U8, align_bytes=64)
        for row in range(ROWS):
            if row == NOTE_ROWS_FIRST:
                nc.sync.dma_start(out=note_words[:].bitcast(I32), in_=notes_words[0].bitcast(I32))
            nc.sync.dma_start(out=note_plane[row:P:QUADRANT, :].bitcast(I32), in_=note_rows[row])
        key_words = sb.tile([P, T], U32, align_bytes=64)
        nc.sync.dma_start(out=key_words[:].bitcast(I32),
                          in_=keys_words[0].rearrange("p n t -> p (n t)").bitcast(I32))
        for row in range(ROWS):
            nc.sync.dma_start(out=key_plane[KEY_ROW + row:P:QUADRANT, :].bitcast(I32), in_=key_rows[row])
        offsets = {}
        for name, src in (("offs2", offs2), ("offs", offs), ("offs3", offs3), ("offs5", offs5), ("offs4", offs4)):
            offsets[name] = lists.tile([P, I // GROUP], U16, name=name)
            nc.sync.dma_start(offsets[name][:], src)

        def half_list(name, h):
            return offsets[name][:, h * HALF // GROUP:(h + 1) * HALF // GROUP]

        q_bf = sb.tile([P, Q, PACK], BF16, name="q_bf", align_bytes=64)
        q_halves = [slice(0, Q // 2), slice(Q // 2, Q)]
        for cols in q_halves:
            nc.vector.tensor_copy(out=q_bf[:, cols, :].rearrange("p (c i) t -> p c t i", i=4),
                                  in_=q_raw[:, :, cols].rearrange("p t (c i) -> p c t i", i=4))
        q_codes = sb.tile([P, Q], U32, align_bytes=64)
        q_plane = sb.tile([P, Q], U8, align_bytes=64)
        for cols in q_halves:
            nc.vector.quantize_mx(out=q_codes[:, cols].bitcast(FP8X4), scales=q_plane[:, cols],
                                  in_=q_bf[:, cols, :].rearrange("p q t -> p (q t)"))

        identity = sb.tile([P, P], F32, name="q_bf", align_bytes=64)
        make_identity(nc, identity[:])

        b = sb.tile([P, U], F32, align_bytes=64)
        for k, c0 in enumerate(range(0, U, PIECE)):
            bank = psum.tile([P, PIECE], F32, name="b_bank%d" % k)
            nc.tensor.matmul_mx(out=bank[:], lhsT=q_codes[:].bitcast(FP8X4), lhsT_scale=q_plane[:],
                                rhs=note_words[:, 2 * c0:2 * (c0 + PIECE)].bitcast(FP4X4),
                                rhs_scale=note_plane[:, c0:c0 + PIECE], start=True, stop=True)
            if k % 2 == 0:
                nc.scalar.activation(b[:, c0:c0 + PIECE], bank[:], COPY)
            else:
                nc.vector.tensor_copy(b[:, c0:c0 + PIECE], bank[:])

        minus_b2 = sb.tile([P, I], F32, align_bytes=64)
        nc.vector.tensor_scalar(minus_b2[:], b[:].indirect(offsets["offs2"][:]), -1.0, 0.0, ALU.mult, ALU.add)
        a = sb.tile([P, T], F32, name="a", align_bytes=64)
        a_banks = []
        for k, c0 in enumerate(range(0, T, PIECE)):
            bank = psum.tile([P, PIECE], F32, name="a_bank%d" % k)
            nc.tensor.matmul_mx(out=bank[:], lhsT=q_codes[:].bitcast(FP8X4), lhsT_scale=q_plane[:],
                                rhs=key_words[:, c0:c0 + PIECE].bitcast(FP8X4),
                                rhs_scale=key_plane[KEY_ROW:P, c0:c0 + PIECE], start=True, stop=True)
            nc.scalar.activation(a[:, c0:c0 + PIECE], bank[:], COPY)
            a_banks.append(bank)

        a1 = sb.tile([P, I], F32, align_bytes=64)
        nc.vector.tensor_copy(a1[:, :HALF], a[:].indirect(half_list("offs", 0)))
        nc.scalar.activation(a1[:, HALF:], a[:].indirect(half_list("offs", 1)), COPY)
        nc.vector.tensor_tensor(f1[:].indirect(offsets["offs3"][:]), a1[:], minus_b2[:], ALU.add)

        beside_scatter = sb.tile([P, I + PIECE], F32, name="a", align_bytes=64)
        b5 = beside_scatter[:, :I]
        a_last = beside_scatter[:, I:]
        nc.scalar.activation(a_last, a_banks[-1][:], COPY)
        nc.scalar.activation(b5, b[:].indirect(offsets["offs5"][:]), COPY)

        r_turned_bank = psum.tile([P, I], F32, name="b_bank0")
        for s0 in range(0, I, P):
            for k, term in enumerate((minus_b2, a1)):
                nc.tensor.matmul(r_turned_bank[:, s0:s0 + P], term[:, s0:s0 + P], identity[:],
                                 start=(k == 0), stop=(k == 1), is_transpose=True)
        r_turned = sb.tile([P, I], F32, name="r_turned", align_bytes=64)
        nc.scalar.activation(r_turned[:], r_turned_bank[:], COPY)
        r = psum.tile([P, I], F32, name="b_bank1")
        for s0 in range(0, I, P):
            nc.tensor.transpose(r[:, s0:s0 + P], r_turned[:, s0:s0 + P], identity[:])

        c1 = sb.tile([P, T], F32, align_bytes=64)
        nc.gpsimd.tensor_tensor(c1[:, T - PIECE:], a_last, f1[:, T - PIECE:], ALU.add)
        for k, c0 in enumerate(range(0, T - PIECE, PIECE)):
            nc.vector.tensor_tensor(c1[:, c0:c0 + PIECE], a_banks[k][:], f1[:, c0:c0 + PIECE], ALU.add)

        c4 = sb.tile([P, I], F32, name="r_turned", align_bytes=64)
        nc.vector.tensor_copy(c4[:, :HALF], c1[:].indirect(half_list("offs4", 0)))
        nc.scalar.activation(c4[:, HALF:], c1[:].indirect(half_list("offs4", 1)), COPY)

        slot_halves = [slice(0, HALF), slice(HALF, I)]
        w = [sb.tile([P, HALF], F32, name="w%d" % h, align_bytes=64) for h in range(2)]
        y = [sb.tile([P, HALF], F32, name="y%d" % h, align_bytes=64) for h in range(2)]
        for h, slots in enumerate(slot_halves):
            nc.vector.tensor_tensor(w[h][:], c4[:, slots], b5[:, slots], ALU.max)
        for h, slots in enumerate(slot_halves):
            nc.vector.tensor_tensor(y[h][:], w[h][:], r[:, slots], ALU.subtract)
            nc.sync.dma_start(out=out[:, slots], in_=y[h][:])
